import numpy as np
import ml_dtypes


def mxq(x, axis, fmt="e4m3"):
    dtype, down = {"e4m3": (ml_dtypes.float8_e4m3fn, 7), "e5m2": (ml_dtypes.float8_e5m2, 14)}[fmt]
    v = np.moveaxis(np.asarray(x, np.float32).astype(ml_dtypes.bfloat16).astype(np.float64), axis, -1)
    blocks = v.reshape(v.shape[:-1] + (-1, 32))
    amax = np.abs(blocks).max(-1, keepdims=True)
    byte = np.maximum(np.where(amax > 0, np.frexp(amax)[1] - 1 + 127, 0) - down, 1)
    scale = np.exp2(byte - 127.0)
    codes = (blocks / scale).astype(np.float32).astype(dtype).astype(np.float64)
    return np.moveaxis((codes * scale).reshape(v.shape), -1, axis)


WIDE = False


def mx_kscale(k):
    if not WIDE:
        return np.ones(k)
    levels = np.array([10, -10, 5, -5, 0])
    if k % 512:
        return np.exp2(np.random.permutation(np.resize(levels, k // 32))).repeat(32)
    a = np.empty((k // 512, 16))
    for p in range(k // 512):
        a[p, :8] = np.random.permutation(np.resize(levels, 8))
        for g in range(8):
            far = levels[np.abs(levels - a[p, g]) >= 10]
            a[p, g + 8] = far[np.random.randint(len(far))]
    return np.exp2(a.ravel()).repeat(32)


def f64(x):
    return np.asarray(x).astype(np.float64)


def striped(idx):
    return np.tile(idx.reshape(-1, 16).T, (8, 1)).astype(np.uint16)


def unstriped(offs):
    return offs[:16].T.reshape(-1).astype(np.int64)


def gelu(v):
    return 0.5 * v * (1.0 + np.tanh(np.sqrt(2.0 / np.pi) * (v + 0.044715 * v**3)))


K, T, E, C, N = 1024, 2048, 4, 256, 256


def by_expert(wq, xq):
    return np.concatenate([wq[e].T @ xq[:, e * C:(e + 1) * C] for e in range(E)], axis=1)


def setup_inputs():
    n = np.random.standard_normal
    s = mx_kscale(K)[:, None]
    return {
        "xT": (n((K, T)) * s).astype(np.float32),
        "w": (n((E, K, N)) / np.sqrt(K) / s[None]).astype(np.float32),
        "b": (0.3 * n((N, E))).astype(np.float32),
        "gate": np.tile(np.random.uniform(0.2, 1.0, E * C), (N, 1)).astype(np.float32),
        "offs": striped(np.random.permutation(T)[:E * C]),
    }


def reference(xT, w, b, gate, offs):
    idx = unstriped(offs)
    xq = mxq(f64(xT)[:, idx], 0, "e4m3")
    y = by_expert(mxq(f64(w), 1, "e4m3"), xq)
    y = gelu(y + np.repeat(f64(b), C, axis=1))
    out = np.zeros((N, T))
    out[:, idx] = f64(gate) * y
    return out

@@ -1,0 +1,187 @@
+from contextlib import ExitStack
+
+import concourse.mybir as mybir
+
+K, T, E, C, N = 1024, 2048, 4, 256, 256
+SLOTS = E * C
+FLOPS = 2 * K * N * SLOTS
+
+F32 = mybir.dt.float32
+BF16 = mybir.dt.bfloat16
+U32 = mybir.dt.uint32
+U16 = mybir.dt.uint16
+U8 = mybir.dt.uint8
+FP8X4 = mybir.dt.float8_e4m3fn_x4
+MULT = mybir.AluOpType.mult
+ADD = mybir.AluOpType.add
+GELU = mybir.ActivationFunctionType.Gelu_apprx_tanh
+COPY = mybir.ActivationFunctionType.Copy
+
+P = 128
+PACK = 4
+K_PASS = P * PACK
+PASSES = K // K_PASS
+NB = N // P
+
+W_ENGINE = ("scalar", "scalar", "scalar", "scalar")
+SCATTER_ORDER = ((0, 0), (0, 1), (1, 0), (1, 1), (2, 0), (3, 0), (2, 1), (3, 1))
+
+
+def tile_routed_moe_kernel(tc, xT, w, b, gate, offs, out):
+    nc = tc.nc
+    with ExitStack() as ctx:
+        lists = ctx.enter_context(tc.tile_pool(name="lists", bufs=1))
+        held = ctx.enter_context(tc.tile_pool(name="held", bufs=1))
+        psum = ctx.enter_context(tc.psum_pool(name="psum", bufs=1))
+
+        offsets = lists.tile([P, SLOTS // 16], U16, name="offsets")
+        nc.sync.dma_start(offsets[:], offs)
+
+        x_planes = xT.rearrange("(g p t) n -> g p t n", p=P, t=PACK)
+        plane = {}
+        for g in range(PASSES):
+            for t in range(PACK):
+                plane[g, t] = held.tile([P, T], F32, name="plane%d%d" % (g, t))
+                nc.sync.dma_start(plane[g, t][:], x_planes[g, :, t, :])
+
+        w_raw = {}
+        bias = held.tile([P, NB, E], F32, name="bias")
+        gate_sb = held.tile([P, NB, SLOTS], F32, name="gate_sb")
+        for e in range(E):
+            w_raw[e] = held.tile([P, PASSES, PACK, N], F32, name="w_raw%d" % e)
+            nc.sync.dma_start(w_raw[e][:], w[e].rearrange("(g p j) n -> p g j n", p=P, j=PACK))
+            if e == 0:
+                nc.sync.dma_start(bias[:], b.rearrange("(h p) e -> p h e", p=P))
+                nc.sync.dma_start(gate_sb[:], gate.rearrange("(h p) j -> p h j", p=P))
+
+        window = {}
+        for h in range(NB):
+            window[h] = held.tile([P, T], F32, name="window%d" % h)
+            nc.vector.memset(window[h][:], 0.0)
+        warm = held.tile([P, 2], F32, name="warm")
+        nc.gpsimd.memset(warm[:, 0:1], 0.0)
+        nc.scalar.activation(out=warm[:, 1:2], in_=warm[:, 0:1], func=GELU)
+
+        g4 = {}
+        x_bf = {}
+        x_q = {}
+        x_s = {}
+        w_q = {}
+        w_s = {}
+        y = {}
+
+        def gather(g, t, c0, nc_):
+            pair = c0 // 2
+            if (g, pair) not in g4:
+                g4[g, pair] = held.tile([P, PACK, 2 * C], F32, name="g4_%d_%d" % (g, pair))
+            lo = (c0 - 2 * pair) * C
+            nc.vector.tensor_copy(
+                g4[g, pair][:, t, lo : lo + nc_ * C],
+                plane[g, t][:].indirect(offsets[:, c0 * (C // 16) : (c0 + nc_) * (C // 16)]),
+            )
+
+        def interleave(g, c0, nc_):
+            pair = c0 // 2
+            lo = (c0 - 2 * pair) * C
+            x_bf[g, c0] = held.tile([P, nc_ * C, PACK], BF16, name="x_bf_%d_%d" % (g, c0), align_bytes=64)
+            nc.scalar.copy(out=x_bf[g, c0][:], in_=g4[g, pair][:, :, lo : lo + nc_ * C].rearrange("p t n -> p n t"))
+
+        def quant_x(g, c0, nc_):
+            x_q[g, c0] = held.tile([P, nc_ * C], U32, name="x_q_%d_%d" % (g, c0), align_bytes=64)
+            x_s[g, c0] = held.tile([P, nc_ * C], U8, name="x_s_%d_%d" % (g, c0), align_bytes=64)
+            nc.vector.quantize_mx(
+                out=x_q[g, c0][:].bitcast(FP8X4),
+                scales=x_s[g, c0][:],
+                in_=x_bf[g, c0][:].rearrange("p n t -> p (n t)"),
+            )
+
+        w_bf = {}
+
+        def interleave_w(e):
+            w_bf[e] = held.tile([P, PASSES, N, PACK], BF16, name="w_bf%d" % e, align_bytes=64)
+            src = w_raw[e][:].rearrange("p g j n -> p g n j")
+            if W_ENGINE[e] == "scalar":
+                nc.scalar.copy(out=w_bf[e][:], in_=src)
+            elif W_ENGINE[e] == "gpsimd":
+                nc.gpsimd.tensor_scalar(w_bf[e][:], src, 1.0, 0.0, MULT, ADD)
+            else:
+                nc.vector.tensor_copy(w_bf[e][:], src)
+
+        def quant_w(e):
+            w_q[e] = held.tile([P, PASSES, N], U32, name="w_q%d" % e, align_bytes=64)
+            w_s[e] = held.tile([P, PASSES, N], U8, name="w_s%d" % e, align_bytes=64)
+            nc.vector.quantize_mx(
+                out=w_q[e][:].rearrange("p g n -> p (g n)").bitcast(FP8X4),
+                scales=w_s[e][:].rearrange("p g n -> p (g n)"),
+                in_=w_bf[e][:].rearrange("p g n j -> p (g n j)"),
+            )
+
+        def operand(g, e):
+            for c0 in range(e, -1, -1):
+                if (g, c0) in x_q:
+                    lo = (e - c0) * C
+                    return x_q[g, c0][:, lo : lo + C], x_s[g, c0][:, lo : lo + C]
+            return None
+
+        def multiply(e):
+            acc = {}
+            for h in range(NB):
+                acc[h] = psum.tile([P, C], F32, name="acc_%d_%d" % (e, h))
+            for g in range(PASSES):
+                codes, scales = operand(g, e)
+                for h in range(NB):
+                    nc.tensor.matmul_mx(
+                        out=acc[h][:],
+                        lhsT=w_q[e][:, g, h * P : (h + 1) * P].bitcast(FP8X4),
+                        lhsT_scale=w_s[e][:, g, h * P : (h + 1) * P],
+                        rhs=codes.bitcast(FP8X4),
+                        rhs_scale=scales,
+                        start=(g == 0),
+                        stop=(g == PASSES - 1),
+                    )
+            for h in range(NB):
+                y[e, h] = held.tile([P, C], F32, name="y_%d_%d" % (e, h))
+                nc.scalar.activation(out=y[e, h][:], in_=acc[h][:], func=GELU, bias=bias[:, h, e : e + 1])
+
+        def scatter(e, h):
+            nc.vector.tensor_tensor(
+                window[h][:].indirect(offsets[:, e * (C // 16) : (e + 1) * (C // 16)]),
+                y[e, h][:],
+                gate_sb[:, h, e * C : (e + 1) * C],
+                MULT,
+            )
+
+        for t in range(PACK):
+            for c0 in (0, 2):
+                gather(0, t, c0, 2)
+        for c0 in (0, 2):
+            interleave(0, c0, 2)
+        for c0 in (0, 2):
+            gather(1, 0, c0, 2)
+        quant_x(0, 0, 2)
+        for c0 in (0, 2):
+            gather(1, 1, c0, 2)
+        quant_x(0, 2, 2)
+        for e in range(E):
+            gather(1, 2, e, 1)
+            gather(1, 3, e, 1)
+            interleave(1, e, 1)
+            if e == 0:
+                interleave_w(0)
+            if e >= 1:
+                quant_x(1, e - 1, 1)
+        quant_w(0)
+        multiply(0)
+        quant_x(1, 3, 1)
+        interleave_w(1)
+        ready = 1
+        for e, h in SCATTER_ORDER:
+            while ready <= e:
+                quant_w(ready)
+                multiply(ready)
+                ready += 1
+                if ready < E:
+                    interleave_w(ready)
+            scatter(e, h)
+            if e == 3:
+                nc.sync.dma_start(out[h * P : (h + 1) * P, :], window[h][:])

@@ -23,8 +23,10 @@ K_PASS = P * PACK
 PASSES = K // K_PASS
 NB = N // P
 
-W_ENGINE = ("scalar", "scalar", "scalar", "scalar")
-SCATTER_ORDER = ((0, 0), (0, 1), (1, 0), (1, 1), (2, 0), (3, 0), (2, 1), (3, 1))
+LOAD_ORDER = (
+    ("x", 0, 0), ("x", 0, 1), ("x", 0, 2), ("x", 0, 3), ("w", 0), ("x", 1, 0), ("x", 1, 1),
+    ("w", 1), ("x", 1, 2), ("x", 1, 3), ("w", 2), ("b",), ("w", 3),
+)
 
 
 def tile_routed_moe_kernel(tc, xT, w, b, gate, offs, out):
@@ -36,23 +38,25 @@ def tile_routed_moe_kernel(tc, xT, w, b, gate, offs, out):
 
         offsets = lists.tile([P, SLOTS // 16], U16, name="offsets")
         nc.sync.dma_start(offsets[:], offs)
+        bias = held.tile([P, NB, E], F32, name="bias")
 
         x_planes = xT.rearrange("(g p t) n -> g p t n", p=P, t=PACK)
-        plane = {}
+        raw = {}
         for g in range(PASSES):
-            for t in range(PACK):
-                plane[g, t] = held.tile([P, T], F32, name="plane%d%d" % (g, t))
-                nc.sync.dma_start(plane[g, t][:], x_planes[g, :, t, :])
-
+            raw[g] = held.tile([P, PACK, T], F32, name="raw%d" % g)
         w_raw = {}
-        bias = held.tile([P, NB, E], F32, name="bias")
-        gate_sb = held.tile([P, NB, SLOTS], F32, name="gate_sb")
-        for e in range(E):
-            w_raw[e] = held.tile([P, PASSES, PACK, N], F32, name="w_raw%d" % e)
-            nc.sync.dma_start(w_raw[e][:], w[e].rearrange("(g p j) n -> p g j n", p=P, j=PACK))
-            if e == 0:
+        for item in LOAD_ORDER:
+            if item[0] == "x":
+                g, t = item[1], item[2]
+                nc.sync.dma_start(raw[g][:, t, :], x_planes[g, :, t, :])
+            elif item[0] == "b":
                 nc.sync.dma_start(bias[:], b.rearrange("(h p) e -> p h e", p=P))
-                nc.sync.dma_start(gate_sb[:], gate.rearrange("(h p) j -> p h j", p=P))
+            else:
+                e = item[1]
+                w_raw[e] = held.tile([P, PASSES, PACK, N], F32, name="w_raw%d" % e)
+                nc.sync.dma_start(w_raw[e][:], w[e].rearrange("(g p j) n -> p g j n", p=P, j=PACK))
+        gate_all = held.tile([P, NB, SLOTS], F32, name="gate_all")
+        nc.sync.dma_start(gate_all[:], gate.rearrange("(h p) j -> p h j", p=P))
 
         window = {}
         for h in range(NB):
@@ -62,50 +66,38 @@ def tile_routed_moe_kernel(tc, xT, w, b, gate, offs, out):
         nc.gpsimd.memset(warm[:, 0:1], 0.0)
         nc.scalar.activation(out=warm[:, 1:2], in_=warm[:, 0:1], func=GELU)
 
-        g4 = {}
         x_bf = {}
         x_q = {}
         x_s = {}
+        w_bf = {}
         w_q = {}
         w_s = {}
         y = {}
+        for pair in range(E // 2):
+            x_bf[pair] = held.tile([P, PASSES, 2 * C, PACK], BF16, name="x_bf%d" % pair, align_bytes=64)
 
-        def gather(g, t, c0, nc_):
-            pair = c0 // 2
-            if (g, pair) not in g4:
-                g4[g, pair] = held.tile([P, PACK, 2 * C], F32, name="g4_%d_%d" % (g, pair))
-            lo = (c0 - 2 * pair) * C
+        def gather(g, t, pair):
             nc.vector.tensor_copy(
-                g4[g, pair][:, t, lo : lo + nc_ * C],
-                plane[g, t][:].indirect(offsets[:, c0 * (C // 16) : (c0 + nc_) * (C // 16)]),
+                x_bf[pair][:, g, :, t],
+                raw[g][:, t, :].indirect(offsets[:, pair * (2 * C // 16) : (pair + 1) * (2 * C // 16)]),
             )
 
-        def interleave(g, c0, nc_):
-            pair = c0 // 2
-            lo = (c0 - 2 * pair) * C
-            x_bf[g, c0] = held.tile([P, nc_ * C, PACK], BF16, name="x_bf_%d_%d" % (g, c0), align_bytes=64)
-            nc.scalar.copy(out=x_bf[g, c0][:], in_=g4[g, pair][:, :, lo : lo + nc_ * C].rearrange("p t n -> p n t"))
-
-        def quant_x(g, c0, nc_):
-            x_q[g, c0] = held.tile([P, nc_ * C], U32, name="x_q_%d_%d" % (g, c0), align_bytes=64)
-            x_s[g, c0] = held.tile([P, nc_ * C], U8, name="x_s_%d_%d" % (g, c0), align_bytes=64)
+        def quant_x(pair):
+            x_q[pair] = held.tile([P, PASSES, 2 * C], U32, name="x_q%d" % pair, align_bytes=64)
+            x_s[pair] = held.tile([P, PASSES, 2 * C], U8, name="x_s%d" % pair, align_bytes=64)
             nc.vector.quantize_mx(
-                out=x_q[g, c0][:].bitcast(FP8X4),
-                scales=x_s[g, c0][:],
-                in_=x_bf[g, c0][:].rearrange("p n t -> p (n t)"),
+                out=x_q[pair][:].rearrange("p g n -> p (g n)").bitcast(FP8X4),
+                scales=x_s[pair][:].rearrange("p g n -> p (g n)"),
+                in_=x_bf[pair][:].rearrange("p g n t -> p (g n t)"),
             )
-
-        w_bf = {}
 
         def interleave_w(e):
             w_bf[e] = held.tile([P, PASSES, N, PACK], BF16, name="w_bf%d" % e, align_bytes=64)
-            src = w_raw[e][:].rearrange("p g j n -> p g n j")
-            if W_ENGINE[e] == "scalar":
-                nc.scalar.copy(out=w_bf[e][:], in_=src)
-            elif W_ENGINE[e] == "gpsimd":
-                nc.gpsimd.tensor_scalar(w_bf[e][:], src, 1.0, 0.0, MULT, ADD)
-            else:
-                nc.vector.tensor_copy(w_bf[e][:], src)
+            for g in range(PASSES):
+                nc.scalar.copy(
+                    out=w_bf[e][:, g].rearrange("p (c i) j -> p c j i", i=4),
+                    in_=w_raw[e][:, g].rearrange("p j (c i) -> p c j i", i=4),
+                )
 
         def quant_w(e):
             w_q[e] = held.tile([P, PASSES, N], U32, name="w_q%d" % e, align_bytes=64)
@@ -116,72 +108,52 @@ def tile_routed_moe_kernel(tc, xT, w, b, gate, offs, out):
                 in_=w_bf[e][:].rearrange("p g n j -> p (g n j)"),
             )
 
-        def operand(g, e):
-            for c0 in range(e, -1, -1):
-                if (g, c0) in x_q:
-                    lo = (e - c0) * C
-                    return x_q[g, c0][:, lo : lo + C], x_s[g, c0][:, lo : lo + C]
-            return None
-
-        def multiply(e):
-            acc = {}
-            for h in range(NB):
-                acc[h] = psum.tile([P, C], F32, name="acc_%d_%d" % (e, h))
+        def multiply(e, h):
+            lo = (e % 2) * C
+            acc = psum.tile([P, C], F32, name="acc_%d_%d" % (e, h))
             for g in range(PASSES):
-                codes, scales = operand(g, e)
-                for h in range(NB):
-                    nc.tensor.matmul_mx(
-                        out=acc[h][:],
-                        lhsT=w_q[e][:, g, h * P : (h + 1) * P].bitcast(FP8X4),
-                        lhsT_scale=w_s[e][:, g, h * P : (h + 1) * P],
-                        rhs=codes.bitcast(FP8X4),
-                        rhs_scale=scales,
-                        start=(g == 0),
-                        stop=(g == PASSES - 1),
-                    )
-            for h in range(NB):
-                y[e, h] = held.tile([P, C], F32, name="y_%d_%d" % (e, h))
-                nc.scalar.activation(out=y[e, h][:], in_=acc[h][:], func=GELU, bias=bias[:, h, e : e + 1])
+                nc.tensor.matmul_mx(
+                    out=acc[:],
+                    lhsT=w_q[e][:, g, h * P : (h + 1) * P].bitcast(FP8X4),
+                    lhsT_scale=w_s[e][:, g, h * P : (h + 1) * P],
+                    rhs=x_q[e // 2][:, g, lo : lo + C].bitcast(FP8X4),
+                    rhs_scale=x_s[e // 2][:, g, lo : lo + C],
+                    start=(g == 0),
+                    stop=(g == PASSES - 1),
+                )
+            y[e, h] = held.tile([P, C], F32, name="y_%d_%d" % (e, h))
+            nc.scalar.activation(out=y[e, h][:], in_=acc[:], func=GELU, bias=bias[:, h, e : e + 1])
 
         def scatter(e, h):
             nc.vector.tensor_tensor(
                 window[h][:].indirect(offsets[:, e * (C // 16) : (e + 1) * (C // 16)]),
                 y[e, h][:],
-                gate_sb[:, h, e * C : (e + 1) * C],
+                gate_all[:, h, e * C : (e + 1) * C],
                 MULT,
             )
 
         for t in range(PACK):
-            for c0 in (0, 2):
-                gather(0, t, c0, 2)
-        for c0 in (0, 2):
-            interleave(0, c0, 2)
-        for c0 in (0, 2):
-            gather(1, 0, c0, 2)
-        quant_x(0, 0, 2)
-        for c0 in (0, 2):
-            gather(1, 1, c0, 2)
-        quant_x(0, 2, 2)
-        for e in range(E):
-            gather(1, 2, e, 1)
-            gather(1, 3, e, 1)
-            interleave(1, e, 1)
-            if e == 0:
-                interleave_w(0)
-            if e >= 1:
-                quant_x(1, e - 1, 1)
+            for pair in range(E // 2):
+                gather(0, t, pair)
+        interleave_w(0)
+        for t in (0, 1):
+            for pair in range(E // 2):
+                gather(1, t, pair)
         quant_w(0)
-        multiply(0)
-        quant_x(1, 3, 1)
         interleave_w(1)
-        ready = 1
-        for e, h in SCATTER_ORDER:
-            while ready <= e:
-                quant_w(ready)
-                multiply(ready)
-                ready += 1
-                if ready < E:
-                    interleave_w(ready)
-            scatter(e, h)
-            if e == 3:
-                nc.sync.dma_start(out[h * P : (h + 1) * P, :], window[h][:])
+        for t in (2, 3):
+            for pair in range(E // 2):
+                gather(1, t, pair)
+        quant_w(1)
+        for pair in range(E // 2):
+            quant_x(pair)
+        for e in (2, 3):
+            interleave_w(e)
+            quant_w(e)
+        for h in range(NB):
+            for e in range(E):
+                multiply(e, h)
+        for h in range(NB):
+            for e in range(E):
+                scatter(e, h)
+            nc.sync.dma_start(out[h * P : (h + 1) * P, :], window[h][:])

@@ -25,8 +25,9 @@ NB = N // P
 
 LOAD_ORDER = (
     ("x", 0, 0), ("x", 0, 1), ("x", 0, 2), ("x", 0, 3), ("w", 0), ("x", 1, 0), ("x", 1, 1),
-    ("w", 1), ("x", 1, 2), ("x", 1, 3), ("w", 2), ("b",), ("w", 3),
+    ("w", 1), ("x", 1, 2), ("x", 1, 3), ("w", 2), ("w", 3),
 )
+W_ENGINE = ("gpsimd", "gpsimd", "scalar", "scalar")
 
 
 def tile_routed_moe_kernel(tc, xT, w, b, gate, offs, out):
@@ -39,18 +40,16 @@ def tile_routed_moe_kernel(tc, xT, w, b, gate, offs, out):
         offsets = lists.tile([P, SLOTS // 16], U16, name="offsets")
         nc.sync.dma_start(offsets[:], offs)
         bias = held.tile([P, NB, E], F32, name="bias")
+        nc.sync.dma_start(bias[:], b.rearrange("(h p) e -> p h e", p=P))
 
         x_planes = xT.rearrange("(g p t) n -> g p t n", p=P, t=PACK)
-        raw = {}
-        for g in range(PASSES):
-            raw[g] = held.tile([P, PACK, T], F32, name="raw%d" % g)
+        plane = {}
         w_raw = {}
         for item in LOAD_ORDER:
             if item[0] == "x":
                 g, t = item[1], item[2]
-                nc.sync.dma_start(raw[g][:, t, :], x_planes[g, :, t, :])
-            elif item[0] == "b":
-                nc.sync.dma_start(bias[:], b.rearrange("(h p) e -> p h e", p=P))
+                plane[g, t] = held.tile([P, T], F32, name="plane%d%d" % (g, t))
+                nc.sync.dma_start(plane[g, t][:], x_planes[g, :, t, :])
             else:
                 e = item[1]
                 w_raw[e] = held.tile([P, PASSES, PACK, N], F32, name="w_raw%d" % e)
@@ -66,6 +65,7 @@ def tile_routed_moe_kernel(tc, xT, w, b, gate, offs, out):
         nc.gpsimd.memset(warm[:, 0:1], 0.0)
         nc.scalar.activation(out=warm[:, 1:2], in_=warm[:, 0:1], func=GELU)
 
+        g4 = {}
         x_bf = {}
         x_q = {}
         x_s = {}
@@ -73,31 +73,47 @@ def tile_routed_moe_kernel(tc, xT, w, b, gate, offs, out):
         w_q = {}
         w_s = {}
         y = {}
-        for pair in range(E // 2):
-            x_bf[pair] = held.tile([P, PASSES, 2 * C, PACK], BF16, name="x_bf%d" % pair, align_bytes=64)
+        for e in range(E):
+            x_bf[e] = held.tile([P, PASSES, C, PACK], BF16, name="x_bf%d" % e, align_bytes=64)
 
-        def gather(g, t, pair):
+        def gather(g, t, e0, n_e):
+            pair = e0 // 2
+            if (g, pair) not in g4:
+                g4[g, pair] = held.tile([P, PACK, 2 * C], F32, name="g4_%d_%d" % (g, pair))
+            lo = (e0 - 2 * pair) * C
             nc.vector.tensor_copy(
-                x_bf[pair][:, g, :, t],
-                raw[g][:, t, :].indirect(offsets[:, pair * (2 * C // 16) : (pair + 1) * (2 * C // 16)]),
+                g4[g, pair][:, t, lo : lo + n_e * C],
+                plane[g, t][:].indirect(offsets[:, e0 * (C // 16) : (e0 + n_e) * (C // 16)]),
             )
 
-        def quant_x(pair):
-            x_q[pair] = held.tile([P, PASSES, 2 * C], U32, name="x_q%d" % pair, align_bytes=64)
-            x_s[pair] = held.tile([P, PASSES, 2 * C], U8, name="x_s%d" % pair, align_bytes=64)
+        def interleave(g, e, t0, n_t):
+            lo = (e % 2) * C
+            nc.scalar.copy(
+                out=x_bf[e][:, g, :, t0 : t0 + n_t].rearrange("p (c i) t -> p c t i", i=4),
+                in_=g4[g, e // 2][:, t0 : t0 + n_t, lo : lo + C].rearrange("p t (c i) -> p c t i", i=4),
+            )
+
+        def quant_x(e):
+            x_q[e] = held.tile([P, PASSES, C], U32, name="x_q%d" % e, align_bytes=64)
+            x_s[e] = held.tile([P, PASSES, C], U8, name="x_s%d" % e, align_bytes=64)
             nc.vector.quantize_mx(
-                out=x_q[pair][:].rearrange("p g n -> p (g n)").bitcast(FP8X4),
-                scales=x_s[pair][:].rearrange("p g n -> p (g n)"),
-                in_=x_bf[pair][:].rearrange("p g n t -> p (g n t)"),
+                out=x_q[e][:].rearrange("p g n -> p (g n)").bitcast(FP8X4),
+                scales=x_s[e][:].rearrange("p g n -> p (g n)"),
+                in_=x_bf[e][:].rearrange("p g n t -> p (g n t)"),
             )
 
         def interleave_w(e):
             w_bf[e] = held.tile([P, PASSES, N, PACK], BF16, name="w_bf%d" % e, align_bytes=64)
             for g in range(PASSES):
-                nc.scalar.copy(
-                    out=w_bf[e][:, g].rearrange("p (c i) j -> p c j i", i=4),
-                    in_=w_raw[e][:, g].rearrange("p j (c i) -> p c j i", i=4),
-                )
+                if W_ENGINE[e] == "scalar":
+                    nc.scalar.copy(
+                        out=w_bf[e][:, g].rearrange("p (c i) j -> p c j i", i=4),
+                        in_=w_raw[e][:, g].rearrange("p j (c i) -> p c j i", i=4),
+                    )
+                else:
+                    nc.gpsimd.tensor_scalar(
+                        w_bf[e][:, g], w_raw[e][:, g].rearrange("p j n -> p n j"), 1.0, 0.0, MULT, ADD
+                    )
 
         def quant_w(e):
             w_q[e] = held.tile([P, PASSES, N], U32, name="w_q%d" % e, align_bytes=64)
@@ -108,21 +124,21 @@ def tile_routed_moe_kernel(tc, xT, w, b, gate, offs, out):
                 in_=w_bf[e][:].rearrange("p g n j -> p (g n j)"),
             )
 
-        def multiply(e, h):
-            lo = (e % 2) * C
-            acc = psum.tile([P, C], F32, name="acc_%d_%d" % (e, h))
-            for g in range(PASSES):
-                nc.tensor.matmul_mx(
-                    out=acc[:],
-                    lhsT=w_q[e][:, g, h * P : (h + 1) * P].bitcast(FP8X4),
-                    lhsT_scale=w_s[e][:, g, h * P : (h + 1) * P],
-                    rhs=x_q[e // 2][:, g, lo : lo + C].bitcast(FP8X4),
-                    rhs_scale=x_s[e // 2][:, g, lo : lo + C],
-                    start=(g == 0),
-                    stop=(g == PASSES - 1),
-                )
-            y[e, h] = held.tile([P, C], F32, name="y_%d_%d" % (e, h))
-            nc.scalar.activation(out=y[e, h][:], in_=acc[:], func=GELU, bias=bias[:, h, e : e + 1])
+        def multiply(e):
+            for h in range(NB):
+                acc = psum.tile([P, C], F32, name="acc_%d_%d" % (e, h))
+                for g in range(PASSES):
+                    nc.tensor.matmul_mx(
+                        out=acc[:],
+                        lhsT=w_q[e][:, g, h * P : (h + 1) * P].bitcast(FP8X4),
+                        lhsT_scale=w_s[e][:, g, h * P : (h + 1) * P],
+                        rhs=x_q[e][:, g, :].bitcast(FP8X4),
+                        rhs_scale=x_s[e][:, g, :],
+                        start=(g == 0),
+                        stop=(g == PASSES - 1),
+                    )
+                y[e, h] = held.tile([P, C], F32, name="y_%d_%d" % (e, h))
+                nc.scalar.activation(out=y[e, h][:], in_=acc[:], func=GELU, bias=bias[:, h, e : e + 1])
 
         def scatter(e, h):
             nc.vector.tensor_tensor(
@@ -133,26 +149,32 @@ def tile_routed_moe_kernel(tc, xT, w, b, gate, offs, out):
             )
 
         for t in range(PACK):
-            for pair in range(E // 2):
-                gather(0, t, pair)
+            for e0 in (0, 2):
+                gather(0, t, e0, 2)
+        for e in range(E):
+            interleave(0, e, 0, PACK)
         interleave_w(0)
-        for t in (0, 1):
-            for pair in range(E // 2):
-                gather(1, t, pair)
         quant_w(0)
+        for t in (0, 1):
+            for e0 in (0, 2):
+                gather(1, t, e0, 2)
+        for e in range(E):
+            interleave(1, e, 0, 2)
         interleave_w(1)
-        for t in (2, 3):
-            for pair in range(E // 2):
-                gather(1, t, pair)
         quant_w(1)
-        for pair in range(E // 2):
-            quant_x(pair)
+        for e0 in (0, 2):
+            gather(1, 2, e0, 2)
+        for e in range(E):
+            gather(1, 3, e, 1)
+            interleave(1, e, 2, 2)
+        for e in range(E):
+            quant_x(e)
+        multiply(0)
+        multiply(1)
         for e in (2, 3):
             interleave_w(e)
             quant_w(e)
-        for h in range(NB):
-            for e in range(E):
-                multiply(e, h)
+            multiply(e)
         for h in range(NB):
             for e in range(E):
                 scatter(e, h)

@@ -24,10 +24,10 @@ PASSES = K // K_PASS
 NB = N // P
 
 LOAD_ORDER = (
-    ("x", 0, 0), ("x", 0, 1), ("x", 0, 2), ("x", 0, 3), ("w", 0), ("x", 1, 0), ("x", 1, 1),
-    ("w", 1), ("x", 1, 2), ("x", 1, 3), ("w", 2), ("w", 3),
+    ("x", 0, 2), ("x", 0, 3), ("x", 1, 0), ("x", 0, 0), ("x", 1, 1), ("x", 0, 1), ("x", 1, 2), ("x", 1, 3),
+    ("w", 0), ("w", 1), ("gate",), ("w", 2), ("w", 3),
 )
-W_ENGINE = ("gpsimd", "gpsimd", "scalar", "scalar")
+S_PLANES = (0, 1)
 
 
 def tile_routed_moe_kernel(tc, xT, w, b, gate, offs, out):
@@ -45,17 +45,18 @@ def tile_routed_moe_kernel(tc, xT, w, b, gate, offs, out):
         x_planes = xT.rearrange("(g p t) n -> g p t n", p=P, t=PACK)
         plane = {}
         w_raw = {}
+        gate_all = held.tile([P, NB, SLOTS], F32, name="gate_all")
         for item in LOAD_ORDER:
             if item[0] == "x":
                 g, t = item[1], item[2]
                 plane[g, t] = held.tile([P, T], F32, name="plane%d%d" % (g, t))
                 nc.sync.dma_start(plane[g, t][:], x_planes[g, :, t, :])
+            elif item[0] == "gate":
+                nc.sync.dma_start(gate_all[:], gate.rearrange("(h p) j -> p h j", p=P))
             else:
                 e = item[1]
                 w_raw[e] = held.tile([P, PASSES, PACK, N], F32, name="w_raw%d" % e)
                 nc.sync.dma_start(w_raw[e][:], w[e].rearrange("(g p j) n -> p g j n", p=P, j=PACK))
-        gate_all = held.tile([P, NB, SLOTS], F32, name="gate_all")
-        nc.sync.dma_start(gate_all[:], gate.rearrange("(h p) j -> p h j", p=P))
 
         window = {}
         for h in range(NB):
@@ -75,11 +76,13 @@ def tile_routed_moe_kernel(tc, xT, w, b, gate, offs, out):
         y = {}
         for e in range(E):
             x_bf[e] = held.tile([P, PASSES, C, PACK], BF16, name="x_bf%d" % e, align_bytes=64)
+        x_16 = held.tile([P, len(S_PLANES), T], BF16, name="x_16")
+        for pair in range(E // 2):
+            g4[0, pair] = held.tile([P, PACK, 2 * C], F32, name="g4_0_%d" % pair)
+            g4[1, pair] = held.tile([P, PACK, 2 * C], F32, name="g4_1_%d" % pair, tag="late%d" % pair, align_bytes=64)
 
         def gather(g, t, e0, n_e):
             pair = e0 // 2
-            if (g, pair) not in g4:
-                g4[g, pair] = held.tile([P, PACK, 2 * C], F32, name="g4_%d_%d" % (g, pair))
             lo = (e0 - 2 * pair) * C
             nc.vector.tensor_copy(
                 g4[g, pair][:, t, lo : lo + n_e * C],
@@ -93,6 +96,16 @@ def tile_routed_moe_kernel(tc, xT, w, b, gate, offs, out):
                 in_=g4[g, e // 2][:, t0 : t0 + n_t, lo : lo + C].rearrange("p t (c i) -> p c t i", i=4),
             )
 
+        def cast_plane(t):
+            nc.gpsimd.tensor_scalar(x_16[:, t, :], plane[0, t][:], 1.0, 0.0, MULT, ADD)
+
+        def gather_scalar(t, e):
+            nc.scalar.activation(
+                out=x_bf[e][:, 0, :, t],
+                in_=x_16[:, t, :].indirect(offsets[:, e * (C // 16) : (e + 1) * (C // 16)]),
+                func=COPY,
+            )
+
         def quant_x(e):
             x_q[e] = held.tile([P, PASSES, C], U32, name="x_q%d" % e, align_bytes=64)
             x_s[e] = held.tile([P, PASSES, C], U8, name="x_s%d" % e, align_bytes=64)
@@ -102,10 +115,10 @@ def tile_routed_moe_kernel(tc, xT, w, b, gate, offs, out):
                 in_=x_bf[e][:].rearrange("p g n t -> p (g n t)"),
             )
 
-        def interleave_w(e):
-            w_bf[e] = held.tile([P, PASSES, N, PACK], BF16, name="w_bf%d" % e, align_bytes=64)
+        def interleave_w(e, engine):
+            w_bf[e] = held.tile([P, PASSES, N, PACK], BF16, name="w_bf%d" % e, tag="w_bf%d" % (e % 2), align_bytes=64)
             for g in range(PASSES):
-                if W_ENGINE[e] == "scalar":
+                if engine == "scalar":
                     nc.scalar.copy(
                         out=w_bf[e][:, g].rearrange("p (c i) j -> p c j i", i=4),
                         in_=w_raw[e][:, g].rearrange("p j (c i) -> p c j i", i=4),
@@ -115,8 +128,8 @@ def tile_routed_moe_kernel(tc, xT, w, b, gate, offs, out):
                         w_bf[e][:, g], w_raw[e][:, g].rearrange("p j n -> p n j"), 1.0, 0.0, MULT, ADD
                     )
 
-        def quant_w(e):
-            w_q[e] = held.tile([P, PASSES, N], U32, name="w_q%d" % e, align_bytes=64)
+        def quant_w(e, tag):
+            w_q[e] = held.tile([P, PASSES, N], U32, name="w_q%d" % e, tag=tag, align_bytes=64)
             w_s[e] = held.tile([P, PASSES, N], U8, name="w_s%d" % e, align_bytes=64)
             nc.vector.quantize_mx(
                 out=w_q[e][:].rearrange("p g n -> p (g n)").bitcast(FP8X4),
@@ -124,21 +137,20 @@ def tile_routed_moe_kernel(tc, xT, w, b, gate, offs, out):
                 in_=w_bf[e][:].rearrange("p g n j -> p (g n j)"),
             )
 
-        def multiply(e):
-            for h in range(NB):
-                acc = psum.tile([P, C], F32, name="acc_%d_%d" % (e, h))
-                for g in range(PASSES):
-                    nc.tensor.matmul_mx(
-                        out=acc[:],
-                        lhsT=w_q[e][:, g, h * P : (h + 1) * P].bitcast(FP8X4),
-                        lhsT_scale=w_s[e][:, g, h * P : (h + 1) * P],
-                        rhs=x_q[e][:, g, :].bitcast(FP8X4),
-                        rhs_scale=x_s[e][:, g, :],
-                        start=(g == 0),
-                        stop=(g == PASSES - 1),
-                    )
-                y[e, h] = held.tile([P, C], F32, name="y_%d_%d" % (e, h))
-                nc.scalar.activation(out=y[e, h][:], in_=acc[:], func=GELU, bias=bias[:, h, e : e + 1])
+        def multiply(e, h):
+            acc = psum.tile([P, C], F32, name="acc_%d_%d" % (e, h))
+            for g in range(PASSES):
+                nc.tensor.matmul_mx(
+                    out=acc[:],
+                    lhsT=w_q[e][:, g, h * P : (h + 1) * P].bitcast(FP8X4),
+                    lhsT_scale=w_s[e][:, g, h * P : (h + 1) * P],
+                    rhs=x_q[e][:, g, :].bitcast(FP8X4),
+                    rhs_scale=x_s[e][:, g, :],
+                    start=(g == 0),
+                    stop=(g == PASSES - 1),
+                )
+            y[e, h] = held.tile([P, C], F32, name="y_%d_%d" % (e, h), tag="y_%d_%d" % (e, h), align_bytes=64)
+            nc.scalar.activation(out=y[e, h][:], in_=acc[:], func=GELU, bias=bias[:, h, e : e + 1])
 
         def scatter(e, h):
             nc.vector.tensor_tensor(
@@ -148,20 +160,26 @@ def tile_routed_moe_kernel(tc, xT, w, b, gate, offs, out):
                 MULT,
             )
 
-        for t in range(PACK):
+        def store(h):
+            nc.sync.dma_start(out[h * P : (h + 1) * P, :], window[h][:])
+
+        for t in (2, 3):
             for e0 in (0, 2):
                 gather(0, t, e0, 2)
         for e in range(E):
-            interleave(0, e, 0, PACK)
-        interleave_w(0)
-        quant_w(0)
-        for t in (0, 1):
-            for e0 in (0, 2):
-                gather(1, t, e0, 2)
+            interleave(0, e, 2, 2)
+        for e0 in (0, 2):
+            gather(1, 0, e0, 2)
+        cast_plane(0)
+        for e in range(E):
+            gather_scalar(0, e)
+        for e0 in (0, 2):
+            gather(1, 1, e0, 2)
         for e in range(E):
             interleave(1, e, 0, 2)
-        interleave_w(1)
-        quant_w(1)
+        cast_plane(1)
+        for e in range(E):
+            gather_scalar(1, e)
         for e0 in (0, 2):
             gather(1, 2, e0, 2)
         for e in range(E):
@@ -169,13 +187,26 @@ def tile_routed_moe_kernel(tc, xT, w, b, gate, offs, out):
             interleave(1, e, 2, 2)
         for e in range(E):
             quant_x(e)
-        multiply(0)
-        multiply(1)
+        for e in (0, 1):
+            interleave_w(e, "gpsimd")
+            quant_w(e, "late%d" % e)
+        for e, h in ((0, 0), (1, 0), (0, 1), (1, 1)):
+            multiply(e, h)
         for e in (2, 3):
-            interleave_w(e)
-            quant_w(e)
-            multiply(e)
-        for h in range(NB):
-            for e in range(E):
-                scatter(e, h)
-            nc.sync.dma_start(out[h * P : (h + 1) * P, :], window[h][:])
+            interleave_w(e, "scalar")
+        scatter(0, 0)
+        scatter(1, 0)
+        scatter(0, 1)
+        quant_w(2, "y_0_1")
+        multiply(2, 0)
+        multiply(2, 1)
+        scatter(1, 1)
+        quant_w(3, "y_1_1")
+        multiply(3, 0)
+        multiply(3, 1)
+        scatter(2, 0)
+        scatter(2, 1)
+        scatter(3, 0)
+        store(0)
+        scatter(3, 1)
+        store(1)

@@ -56,7 +56,12 @@ def tile_routed_moe_kernel(tc, xT, w, b, gate, offs, out):
             else:
                 e = item[1]
                 w_raw[e] = held.tile([P, PASSES, PACK, N], F32, name="w_raw%d" % e)
-                nc.sync.dma_start(w_raw[e][:], w[e].rearrange("(g p j) n -> p g j n", p=P, j=PACK))
+                w_view = w[e].rearrange("(g p j) n -> p g j n", p=P, j=PACK)
+                if e == 0:
+                    for g in range(PASSES):
+                        nc.sync.dma_start(w_raw[e][:, g], w_view[:, g])
+                else:
+                    nc.sync.dma_start(w_raw[e][:], w_view)
 
         window = {}
         for h in range(NB):
@@ -89,9 +94,10 @@ def tile_routed_moe_kernel(tc, xT, w, b, gate, offs, out):
                 plane[g, t][:].indirect(offsets[:, e0 * (C // 16) : (e0 + n_e) * (C // 16)]),
             )
 
-        def interleave(g, e, t0, n_t):
+        def interleave(g, e, t0, n_t, engine="scalar"):
             lo = (e % 2) * C
-            nc.scalar.copy(
+            copy = nc.vector.tensor_copy if engine == "vector" else nc.scalar.copy
+            copy(
                 out=x_bf[e][:, g, :, t0 : t0 + n_t].rearrange("p (c i) t -> p c t i", i=4),
                 in_=g4[g, e // 2][:, t0 : t0 + n_t, lo : lo + C].rearrange("p t (c i) -> p c t i", i=4),
             )
@@ -176,7 +182,7 @@ def tile_routed_moe_kernel(tc, xT, w, b, gate, offs, out):
         for e0 in (0, 2):
             gather(1, 1, e0, 2)
         for e in range(E):
-            interleave(1, e, 0, 2)
+            interleave(1, e, 0, 2, "vector")
         cast_plane(1)
         for e in range(E):
             gather_scalar(1, e)

@@ -24,7 +24,7 @@ PASSES = K // K_PASS
 NB = N // P
 
 LOAD_ORDER = (
-    ("x", 0, 2), ("x", 0, 3), ("x", 1, 0), ("x", 0, 0), ("x", 1, 1), ("x", 0, 1), ("x", 1, 2), ("x", 1, 3),
+    ("x", 0, 2), ("x", 0, 3), ("x", 1, 0), ("x", 0, 0), ("x", 0, 1), ("x", 1, 1), ("x", 1, 2), ("x", 1, 3),
     ("w", 0), ("w", 1), ("gate",), ("w", 2), ("w", 3),
 )
 S_PLANES = (0, 1)
@@ -76,34 +76,45 @@ def tile_routed_moe_kernel(tc, xT, w, b, gate, offs, out):
         x_q = {}
         x_s = {}
         w_bf = {}
+        w_bf_whole = {}
         w_q = {}
         w_s = {}
         y = {}
         for e in range(E):
-            x_bf[e] = held.tile([P, PASSES, C, PACK], BF16, name="x_bf%d" % e, align_bytes=64)
+            x_bf[e] = held.tile([P, PASSES, C, PACK], BF16, name="x_bf%d" % e, tag="x_bf%d" % e, align_bytes=64)
         x_16 = held.tile([P, len(S_PLANES), T], BF16, name="x_16")
         for pair in range(E // 2):
-            g4[0, pair] = held.tile([P, PACK, 2 * C], F32, name="g4_0_%d" % pair)
-            g4[1, pair] = held.tile([P, PACK, 2 * C], F32, name="g4_1_%d" % pair, tag="late%d" % pair, align_bytes=64)
+            g4[0, 1, pair] = held.tile([P, 2, 2 * C], F32, name="g4_0_1_%d" % pair)
+            g4[1, 0, pair] = held.tile([P, 2, 2 * C], F32, name="g4_1_0_%d" % pair)
+            g4[1, 1, pair] = held.tile([P, 2, 2 * C], F32, name="g4_1_1_%d" % pair, tag="late%d" % pair, align_bytes=64)
 
         def gather(g, t, e0, n_e):
             pair = e0 // 2
             lo = (e0 - 2 * pair) * C
             nc.vector.tensor_copy(
-                g4[g, pair][:, t, lo : lo + n_e * C],
+                g4[g, t // 2, pair][:, t % 2, lo : lo + n_e * C],
                 plane[g, t][:].indirect(offsets[:, e0 * (C // 16) : (e0 + n_e) * (C // 16)]),
             )
 
         def interleave(g, e, t0, n_t, engine="scalar"):
             lo = (e % 2) * C
-            copy = nc.vector.tensor_copy if engine == "vector" else nc.scalar.copy
-            copy(
-                out=x_bf[e][:, g, :, t0 : t0 + n_t].rearrange("p (c i) t -> p c t i", i=4),
-                in_=g4[g, e // 2][:, t0 : t0 + n_t, lo : lo + C].rearrange("p t (c i) -> p c t i", i=4),
-            )
+            if engine == "gpsimd":
+                nc.gpsimd.tensor_scalar(
+                    x_bf[e][:, g, :, t0 : t0 + n_t],
+                    g4[g, t0 // 2, e // 2][:, :, lo : lo + C].rearrange("p t c -> p c t"),
+                    1.0,
+                    0.0,
+                    MULT,
+                    ADD,
+                )
+            else:
+                nc.scalar.copy(
+                    out=x_bf[e][:, g, :, t0 : t0 + n_t].rearrange("p (c i) t -> p c t i", i=4),
+                    in_=g4[g, t0 // 2, e // 2][:, :, lo : lo + C].rearrange("p t (c i) -> p c t i", i=4),
+                )
 
         def cast_plane(t):
-            nc.gpsimd.tensor_scalar(x_16[:, t, :], plane[0, t][:], 1.0, 0.0, MULT, ADD)
+            nc.vector.tensor_copy(x_16[:, t, :], plane[0, t][:])
 
         def gather_scalar(t, e):
             nc.scalar.activation(
@@ -121,27 +132,45 @@ def tile_routed_moe_kernel(tc, xT, w, b, gate, offs, out):
                 in_=x_bf[e][:].rearrange("p g n t -> p (g n t)"),
             )
 
-        def interleave_w(e, engine):
-            w_bf[e] = held.tile([P, PASSES, N, PACK], BF16, name="w_bf%d" % e, tag="w_bf%d" % (e % 2), align_bytes=64)
+        def interleave_w(e, engines, tags):
+            if tags[0] == tags[1]:
+                whole = held.tile([P, PASSES, N, PACK], BF16, name="w_bf%d" % e, tag=tags[0], align_bytes=64)
+                w_bf[e] = [whole[:, g] for g in range(PASSES)]
+                w_bf_whole[e] = whole
+            else:
+                halves = [
+                    held.tile([P, N, PACK], BF16, name="w_bf%d_%d" % (e, g), tag=tags[g], align_bytes=64)
+                    for g in range(PASSES)
+                ]
+                w_bf[e] = [half[:] for half in halves]
             for g in range(PASSES):
-                if engine == "scalar":
-                    nc.scalar.copy(
-                        out=w_bf[e][:, g].rearrange("p (c i) j -> p c j i", i=4),
+                if engines[g] != "gpsimd":
+                    copy = nc.vector.tensor_copy if engines[g] == "vector" else nc.scalar.copy
+                    copy(
+                        out=w_bf[e][g].rearrange("p (c i) j -> p c j i", i=4),
                         in_=w_raw[e][:, g].rearrange("p j (c i) -> p c j i", i=4),
                     )
                 else:
                     nc.gpsimd.tensor_scalar(
-                        w_bf[e][:, g], w_raw[e][:, g].rearrange("p j n -> p n j"), 1.0, 0.0, MULT, ADD
+                        w_bf[e][g], w_raw[e][:, g].rearrange("p j n -> p n j"), 1.0, 0.0, MULT, ADD
                     )
 
         def quant_w(e, tag):
             w_q[e] = held.tile([P, PASSES, N], U32, name="w_q%d" % e, tag=tag, align_bytes=64)
             w_s[e] = held.tile([P, PASSES, N], U8, name="w_s%d" % e, align_bytes=64)
-            nc.vector.quantize_mx(
-                out=w_q[e][:].rearrange("p g n -> p (g n)").bitcast(FP8X4),
-                scales=w_s[e][:].rearrange("p g n -> p (g n)"),
-                in_=w_bf[e][:].rearrange("p g n j -> p (g n j)"),
-            )
+            if e in w_bf_whole:
+                nc.vector.quantize_mx(
+                    out=w_q[e][:].rearrange("p g n -> p (g n)").bitcast(FP8X4),
+                    scales=w_s[e][:].rearrange("p g n -> p (g n)"),
+                    in_=w_bf_whole[e][:].rearrange("p g n j -> p (g n j)"),
+                )
+            else:
+                for g in range(PASSES):
+                    nc.vector.quantize_mx(
+                        out=w_q[e][:, g, :].bitcast(FP8X4),
+                        scales=w_s[e][:, g, :],
+                        in_=w_bf[e][g].rearrange("p n j -> p (n j)"),
+                    )
 
         def multiply(e, h):
             acc = psum.tile([P, C], F32, name="acc_%d_%d" % (e, h))
@@ -179,13 +208,13 @@ def tile_routed_moe_kernel(tc, xT, w, b, gate, offs, out):
         cast_plane(0)
         for e in range(E):
             gather_scalar(0, e)
-        for e0 in (0, 2):
-            gather(1, 1, e0, 2)
-        for e in range(E):
-            interleave(1, e, 0, 2, "vector")
         cast_plane(1)
         for e in range(E):
             gather_scalar(1, e)
+        for e0 in (0, 2):
+            gather(1, 1, e0, 2)
+        for e in range(E):
+            interleave(1, e, 0, 2, "gpsimd")
         for e0 in (0, 2):
             gather(1, 2, e0, 2)
         for e in range(E):
@@ -193,13 +222,14 @@ def tile_routed_moe_kernel(tc, xT, w, b, gate, offs, out):
             interleave(1, e, 2, 2)
         for e in range(E):
             quant_x(e)
-        for e in (0, 1):
-            interleave_w(e, "gpsimd")
-            quant_w(e, "late%d" % e)
+        interleave_w(0, ("gpsimd", "scalar"), ("w_bf0", "late1"))
+        quant_w(0, "late0")
+        interleave_w(1, ("vector", "vector"), ("late1", "late1"))
+        quant_w(1, "x_bf3")
         for e, h in ((0, 0), (1, 0), (0, 1), (1, 1)):
             multiply(e, h)
         for e in (2, 3):
-            interleave_w(e, "scalar")
+            interleave_w(e, ("scalar", "scalar"), ("w_bf%d" % (e % 2), "w_bf%d" % (e % 2)))
         scatter(0, 0)
         scatter(1, 0)
         scatter(0, 1)

@@ -24,8 +24,8 @@ PASSES = K // K_PASS
 NB = N // P
 
 LOAD_ORDER = (
-    ("x", 0, 2), ("x", 0, 3), ("x", 1, 0), ("x", 0, 0), ("x", 0, 1), ("x", 1, 1), ("x", 1, 2), ("x", 1, 3),
-    ("w", 0), ("w", 1), ("gate",), ("w", 2), ("w", 3),
+    ("x", 0, 2), ("offs",), ("x", 0, 3), ("x", 1, 0), ("x", 0, 0), ("x", 0, 1), ("x", 1, 1), ("x", 1, 2), ("x", 1, 3),
+    ("w", 0), ("bias",), ("w", 1), ("gate",), ("w", 2), ("w", 3),
 )
 S_PLANES = (0, 1)
 
@@ -38,9 +38,7 @@ def tile_routed_moe_kernel(tc, xT, w, b, gate, offs, out):
         psum = ctx.enter_context(tc.psum_pool(name="psum", bufs=1))
 
         offsets = lists.tile([P, SLOTS // 16], U16, name="offsets")
-        nc.sync.dma_start(offsets[:], offs)
         bias = held.tile([P, NB, E], F32, name="bias")
-        nc.sync.dma_start(bias[:], b.rearrange("(h p) e -> p h e", p=P))
 
         x_planes = xT.rearrange("(g p t) n -> g p t n", p=P, t=PACK)
         plane = {}
@@ -51,11 +49,15 @@ def tile_routed_moe_kernel(tc, xT, w, b, gate, offs, out):
                 g, t = item[1], item[2]
                 plane[g, t] = held.tile([P, T], F32, name="plane%d%d" % (g, t))
                 nc.sync.dma_start(plane[g, t][:], x_planes[g, :, t, :])
+            elif item[0] == "offs":
+                nc.sync.dma_start(offsets[:], offs)
+            elif item[0] == "bias":
+                nc.sync.dma_start(bias[:], b.rearrange("(h p) e -> p h e", p=P))
             elif item[0] == "gate":
                 nc.sync.dma_start(gate_all[:], gate.rearrange("(h p) j -> p h j", p=P))
             else:
                 e = item[1]
-                w_raw[e] = held.tile([P, PASSES, PACK, N], F32, name="w_raw%d" % e)
+                w_raw[e] = held.tile([P, PASSES, PACK, N], F32, name="w_raw%d" % e, tag="w_raw%d" % e, align_bytes=64)
                 w_view = w[e].rearrange("(g p j) n -> p g j n", p=P, j=PACK)
                 if e == 0:
                     for g in range(PASSES):
@@ -80,13 +82,16 @@ def tile_routed_moe_kernel(tc, xT, w, b, gate, offs, out):
         w_q = {}
         w_s = {}
         y = {}
+        y_tag = {(0, 1): "w_raw2", (1, 1): "w_raw3"}
+        y_pair = [held.tile([P, 2 * C], F32, name="y_pair%d" % h) for h in range(NB)]
         for e in range(E):
             x_bf[e] = held.tile([P, PASSES, C, PACK], BF16, name="x_bf%d" % e, tag="x_bf%d" % e, align_bytes=64)
         x_16 = held.tile([P, len(S_PLANES), T], BF16, name="x_16")
         for pair in range(E // 2):
             g4[0, 1, pair] = held.tile([P, 2, 2 * C], F32, name="g4_0_1_%d" % pair)
-            g4[1, 0, pair] = held.tile([P, 2, 2 * C], F32, name="g4_1_0_%d" % pair)
             g4[1, 1, pair] = held.tile([P, 2, 2 * C], F32, name="g4_1_1_%d" % pair, tag="late%d" % pair, align_bytes=64)
+
+        g4_all = held.tile([P, 2, SLOTS], F32, name="g4_all")
 
         def gather(g, t, e0, n_e):
             pair = e0 // 2
@@ -96,12 +101,15 @@ def tile_routed_moe_kernel(tc, xT, w, b, gate, offs, out):
                 plane[g, t][:].indirect(offsets[:, e0 * (C // 16) : (e0 + n_e) * (C // 16)]),
             )
 
+        def gather_all(t):
+            nc.vector.tensor_copy(g4_all[:, t, :], plane[1, t][:].indirect(offsets[:]))
+
         def interleave(g, e, t0, n_t, engine="scalar"):
             lo = (e % 2) * C
             if engine == "gpsimd":
                 nc.gpsimd.tensor_scalar(
                     x_bf[e][:, g, :, t0 : t0 + n_t],
-                    g4[g, t0 // 2, e // 2][:, :, lo : lo + C].rearrange("p t c -> p c t"),
+                    g4_all[:, :, e * C : (e + 1) * C].rearrange("p t c -> p c t"),
                     1.0,
                     0.0,
                     MULT,
@@ -184,14 +192,26 @@ def tile_routed_moe_kernel(tc, xT, w, b, gate, offs, out):
                     start=(g == 0),
                     stop=(g == PASSES - 1),
                 )
-            y[e, h] = held.tile([P, C], F32, name="y_%d_%d" % (e, h), tag="y_%d_%d" % (e, h), align_bytes=64)
-            nc.scalar.activation(out=y[e, h][:], in_=acc[:], func=GELU, bias=bias[:, h, e : e + 1])
+            if e < 2:
+                y_tile = held.tile([P, C], F32, name="y_%d_%d" % (e, h), tag=y_tag.get((e, h), "y_%d_%d" % (e, h)), align_bytes=64)
+                y[e, h] = y_tile[:]
+            else:
+                y[e, h] = y_pair[h][:, (e - 2) * C : (e - 1) * C]
+            nc.scalar.activation(out=y[e, h], in_=acc[:], func=GELU, bias=bias[:, h, e : e + 1])
 
         def scatter(e, h):
             nc.vector.tensor_tensor(
                 window[h][:].indirect(offsets[:, e * (C // 16) : (e + 1) * (C // 16)]),
-                y[e, h][:],
+                y[e, h],
                 gate_all[:, h, e * C : (e + 1) * C],
+                MULT,
+            )
+
+        def scatter_pair(h):
+            nc.vector.tensor_tensor(
+                window[h][:].indirect(offsets[:, 2 * (C // 16) : 4 * (C // 16)]),
+                y_pair[h][:],
+                gate_all[:, h, 2 * C : 4 * C],
                 MULT,
             )
 
@@ -203,16 +223,14 @@ def tile_routed_moe_kernel(tc, xT, w, b, gate, offs, out):
                 gather(0, t, e0, 2)
         for e in range(E):
             interleave(0, e, 2, 2)
-        for e0 in (0, 2):
-            gather(1, 0, e0, 2)
+        gather_all(0)
         cast_plane(0)
         for e in range(E):
             gather_scalar(0, e)
         cast_plane(1)
         for e in range(E):
             gather_scalar(1, e)
-        for e0 in (0, 2):
-            gather(1, 1, e0, 2)
+        gather_all(1)
         for e in range(E):
             interleave(1, e, 0, 2, "gpsimd")
         for e0 in (0, 2):
@@ -226,23 +244,23 @@ def tile_routed_moe_kernel(tc, xT, w, b, gate, offs, out):
         quant_w(0, "late0")
         interleave_w(1, ("vector", "vector"), ("late1", "late1"))
         quant_w(1, "x_bf3")
-        for e, h in ((0, 0), (1, 0), (0, 1), (1, 1)):
-            multiply(e, h)
+        multiply(0, 0)
+        multiply(1, 0)
         for e in (2, 3):
             interleave_w(e, ("scalar", "scalar"), ("w_bf%d" % (e % 2), "w_bf%d" % (e % 2)))
         scatter(0, 0)
         scatter(1, 0)
-        scatter(0, 1)
-        quant_w(2, "y_0_1")
+        quant_w(2, "y_1_0")
+        multiply(0, 1)
         multiply(2, 0)
         multiply(2, 1)
-        scatter(1, 1)
-        quant_w(3, "y_1_1")
+        scatter(0, 1)
+        quant_w(3, "y_0_0")
+        multiply(1, 1)
         multiply(3, 0)
         multiply(3, 1)
-        scatter(2, 0)
-        scatter(2, 1)
-        scatter(3, 0)
+        scatter(1, 1)
+        scatter_pair(0)
         store(0)
-        scatter(3, 1)
+        scatter_pair(1)
         store(1)

@@ -122,7 +122,7 @@ def tile_routed_moe_kernel(tc, xT, w, b, gate, offs, out):
                 )
 
         def cast_plane(t):
-            nc.vector.tensor_copy(x_16[:, t, :], plane[0, t][:])
+            nc.gpsimd.tensor_scalar(x_16[:, t, :], plane[0, t][:], 1.0, 0.0, MULT, ADD)
 
         def gather_scalar(t, e):
             nc.scalar.activation(

@@ -57,13 +57,19 @@ def tile_routed_moe_kernel(tc, xT, w, b, gate, offs, out):
                 nc.sync.dma_start(gate_all[:], gate.rearrange("(h p) j -> p h j", p=P))
             else:
                 e = item[1]
-                w_raw[e] = held.tile([P, PASSES, PACK, N], F32, name="w_raw%d" % e, tag="w_raw%d" % e, align_bytes=64)
                 w_view = w[e].rearrange("(g p j) n -> p g j n", p=P, j=PACK)
-                if e == 0:
+                if e < 2:
                     for g in range(PASSES):
-                        nc.sync.dma_start(w_raw[e][:, g], w_view[:, g])
+                        half = held.tile(
+                            [P, PACK, N], F32, name="w_raw%d_%d" % (e, g), tag="w_raw%d_%d" % (e, g), align_bytes=64
+                        )
+                        nc.sync.dma_start(half[:], w_view[:, g])
+                        w_raw[e, g] = half[:]
                 else:
-                    nc.sync.dma_start(w_raw[e][:], w_view)
+                    whole = held.tile([P, PASSES, PACK, N], F32, name="w_raw%d" % e, tag="w_raw%d" % e, align_bytes=64)
+                    nc.sync.dma_start(whole[:], w_view)
+                    for g in range(PASSES):
+                        w_raw[e, g] = whole[:, g]
 
         window = {}
         for h in range(NB):
@@ -82,7 +88,7 @@ def tile_routed_moe_kernel(tc, xT, w, b, gate, offs, out):
         w_q = {}
         w_s = {}
         y = {}
-        y_tag = {(0, 1): "w_raw2", (1, 1): "w_raw3"}
+        y_tag = {(0, 0): "w_raw1_0", (0, 1): "w_raw1_1", (1, 0): "w_raw2", (1, 1): "w_raw3"}
         y_pair = [held.tile([P, 2 * C], F32, name="y_pair%d" % h) for h in range(NB)]
         for e in range(E):
             x_bf[e] = held.tile([P, PASSES, C, PACK], BF16, name="x_bf%d" % e, tag="x_bf%d" % e, align_bytes=64)
@@ -140,7 +146,7 @@ def tile_routed_moe_kernel(tc, xT, w, b, gate, offs, out):
                 in_=x_bf[e][:].rearrange("p g n t -> p (g n t)"),
             )
 
-        def interleave_w(e, engines, tags):
+        def alloc_w_bf(e, tags):
             if tags[0] == tags[1]:
                 whole = held.tile([P, PASSES, N, PACK], BF16, name="w_bf%d" % e, tag=tags[0], align_bytes=64)
                 w_bf[e] = [whole[:, g] for g in range(PASSES)]
@@ -151,17 +157,15 @@ def tile_routed_moe_kernel(tc, xT, w, b, gate, offs, out):
                     for g in range(PASSES)
                 ]
                 w_bf[e] = [half[:] for half in halves]
-            for g in range(PASSES):
-                if engines[g] != "gpsimd":
-                    copy = nc.vector.tensor_copy if engines[g] == "vector" else nc.scalar.copy
-                    copy(
-                        out=w_bf[e][g].rearrange("p (c i) j -> p c j i", i=4),
-                        in_=w_raw[e][:, g].rearrange("p j (c i) -> p c j i", i=4),
-                    )
-                else:
-                    nc.gpsimd.tensor_scalar(
-                        w_bf[e][g], w_raw[e][:, g].rearrange("p j n -> p n j"), 1.0, 0.0, MULT, ADD
-                    )
+
+        def copy_w(e, g, engine):
+            if engine == "scalar":
+                nc.scalar.copy(
+                    out=w_bf[e][g].rearrange("p (c i) j -> p c j i", i=4),
+                    in_=w_raw[e, g].rearrange("p j (c i) -> p c j i", i=4),
+                )
+            else:
+                nc.gpsimd.tensor_scalar(w_bf[e][g], w_raw[e, g].rearrange("p j n -> p n j"), 1.0, 0.0, MULT, ADD)
 
         def quant_w(e, tag):
             w_q[e] = held.tile([P, PASSES, N], U32, name="w_q%d" % e, tag=tag, align_bytes=64)
@@ -240,23 +244,31 @@ def tile_routed_moe_kernel(tc, xT, w, b, gate, offs, out):
             interleave(1, e, 2, 2)
         for e in range(E):
             quant_x(e)
-        interleave_w(0, ("gpsimd", "scalar"), ("w_bf0", "late1"))
+        alloc_w_bf(0, ("w_bf0", "late1"))
+        copy_w(0, 0, "gpsimd")
+        copy_w(0, 1, "scalar")
         quant_w(0, "late0")
-        interleave_w(1, ("vector", "vector"), ("late1", "late1"))
-        quant_w(1, "x_bf3")
+        alloc_w_bf(1, ("x_bf0", "x_bf0"))
+        copy_w(1, 0, "scalar")
         multiply(0, 0)
-        multiply(1, 0)
-        for e in (2, 3):
-            interleave_w(e, ("scalar", "scalar"), ("w_bf%d" % (e % 2), "w_bf%d" % (e % 2)))
-        scatter(0, 0)
-        scatter(1, 0)
-        quant_w(2, "y_1_0")
+        copy_w(1, 1, "scalar")
         multiply(0, 1)
+        scatter(0, 0)
+        quant_w(1, "x_bf3")
+        alloc_w_bf(2, ("w_bf0", "w_bf0"))
+        copy_w(2, 0, "scalar")
+        copy_w(2, 1, "scalar")
+        multiply(1, 0)
+        scatter(0, 1)
+        quant_w(2, "x_bf1")
+        alloc_w_bf(3, ("w_bf1", "w_bf1"))
+        copy_w(3, 0, "scalar")
+        copy_w(3, 1, "scalar")
+        multiply(1, 1)
+        scatter(1, 0)
+        quant_w(3, "x_bf2")
         multiply(2, 0)
         multiply(2, 1)
-        scatter(0, 1)
-        quant_w(3, "y_0_0")
-        multiply(1, 1)
         multiply(3, 0)
         multiply(3, 1)
         scatter(1, 1)

@@ -93,29 +93,22 @@ def tile_routed_moe_kernel(tc, xT, w, b, gate, offs, out):
         for e in range(E):
             x_bf[e] = held.tile([P, PASSES, C, PACK], BF16, name="x_bf%d" % e, tag="x_bf%d" % e, align_bytes=64)
         x_16 = held.tile([P, len(S_PLANES), T], BF16, name="x_16")
-        for pair in range(E // 2):
-            g4[0, 1, pair] = held.tile([P, 2, 2 * C], F32, name="g4_0_1_%d" % pair)
-            g4[1, 1, pair] = held.tile([P, 2, 2 * C], F32, name="g4_1_1_%d" % pair, tag="late%d" % pair, align_bytes=64)
-
-        g4_all = held.tile([P, 2, SLOTS], F32, name="g4_all")
+        g4[0, 1] = held.tile([P, 2, SLOTS], F32, name="g4_0_1")
+        g4[1, 0] = held.tile([P, 2, SLOTS], F32, name="g4_1_0")
+        g4[1, 1] = held.tile([P, 2, SLOTS], F32, name="g4_1_1", tag="late", align_bytes=64)
 
         def gather(g, t, e0, n_e):
-            pair = e0 // 2
-            lo = (e0 - 2 * pair) * C
             nc.vector.tensor_copy(
-                g4[g, t // 2, pair][:, t % 2, lo : lo + n_e * C],
+                g4[g, t // 2][:, t % 2, e0 * C : (e0 + n_e) * C],
                 plane[g, t][:].indirect(offsets[:, e0 * (C // 16) : (e0 + n_e) * (C // 16)]),
             )
 
-        def gather_all(t):
-            nc.vector.tensor_copy(g4_all[:, t, :], plane[1, t][:].indirect(offsets[:]))
-
         def interleave(g, e, t0, n_t, engine="scalar"):
-            lo = (e % 2) * C
+            picked = g4[g, t0 // 2][:, :, e * C : (e + 1) * C]
             if engine == "gpsimd":
                 nc.gpsimd.tensor_scalar(
                     x_bf[e][:, g, :, t0 : t0 + n_t],
-                    g4_all[:, :, e * C : (e + 1) * C].rearrange("p t c -> p c t"),
+                    picked.rearrange("p t c -> p c t"),
                     1.0,
                     0.0,
                     MULT,
@@ -124,7 +117,7 @@ def tile_routed_moe_kernel(tc, xT, w, b, gate, offs, out):
             else:
                 nc.scalar.copy(
                     out=x_bf[e][:, g, :, t0 : t0 + n_t].rearrange("p (c i) t -> p c t i", i=4),
-                    in_=g4[g, t0 // 2, e // 2][:, :, lo : lo + C].rearrange("p t (c i) -> p c t i", i=4),
+                    in_=picked.rearrange("p t (c i) -> p c t i", i=4),
                 )
 
         def cast_plane(t):
@@ -223,32 +216,30 @@ def tile_routed_moe_kernel(tc, xT, w, b, gate, offs, out):
             nc.sync.dma_start(out[h * P : (h + 1) * P, :], window[h][:])
 
         for t in (2, 3):
-            for e0 in (0, 2):
-                gather(0, t, e0, 2)
+            gather(0, t, 0, E)
         for e in range(E):
             interleave(0, e, 2, 2)
-        gather_all(0)
+        gather(1, 0, 0, E)
         cast_plane(0)
         for e in range(E):
             gather_scalar(0, e)
         cast_plane(1)
         for e in range(E):
             gather_scalar(1, e)
-        gather_all(1)
+        gather(1, 1, 0, E)
         for e in range(E):
             interleave(1, e, 0, 2, "gpsimd")
-        for e0 in (0, 2):
-            gather(1, 2, e0, 2)
+        gather(1, 2, 0, E)
         for e in range(E):
             gather(1, 3, e, 1)
             interleave(1, e, 2, 2)
         for e in range(E):
             quant_x(e)
-        alloc_w_bf(0, ("w_bf0", "late1"))
+        alloc_w_bf(0, ("w_bf0", "late"))
         copy_w(0, 0, "gpsimd")
         copy_w(0, 1, "scalar")
-        quant_w(0, "late0")
-        alloc_w_bf(1, ("x_bf0", "x_bf0"))
+        quant_w(0, "w_q0")
+        alloc_w_bf(1, ("x_bf0", "x_bf1"))
         copy_w(1, 0, "scalar")
         multiply(0, 0)
         copy_w(1, 1, "scalar")
@@ -260,7 +251,7 @@ def tile_routed_moe_kernel(tc, xT, w, b, gate, offs, out):
         copy_w(2, 1, "scalar")
         multiply(1, 0)
         scatter(0, 1)
-        quant_w(2, "x_bf1")
+        quant_w(2, "w_q2")
         alloc_w_bf(3, ("w_bf1", "w_bf1"))
         copy_w(3, 0, "scalar")
         copy_w(3, 1, "scalar")

@@ -25,7 +25,7 @@ NB = N // P
 
 LOAD_ORDER = (
     ("x", 0, 2), ("offs",), ("x", 0, 3), ("x", 1, 0), ("x", 0, 0), ("x", 0, 1), ("x", 1, 1), ("x", 1, 2), ("x", 1, 3),
-    ("w", 0), ("bias",), ("w", 1), ("gate",), ("w", 2), ("w", 3),
+    ("w", 0), ("bias",), ("gate", 0), ("w", 1), ("w", 2), ("w", 3), ("gate", 1),
 )
 S_PLANES = (0, 1)
 
@@ -43,7 +43,7 @@ def tile_routed_moe_kernel(tc, xT, w, b, gate, offs, out):
         x_planes = xT.rearrange("(g p t) n -> g p t n", p=P, t=PACK)
         plane = {}
         w_raw = {}
-        gate_all = held.tile([P, NB, SLOTS], F32, name="gate_all")
+        gate_pair = [held.tile([P, NB, 2 * C], F32, name="gate_pair%d" % q) for q in range(E // 2)]
         for item in LOAD_ORDER:
             if item[0] == "x":
                 g, t = item[1], item[2]
@@ -54,22 +54,17 @@ def tile_routed_moe_kernel(tc, xT, w, b, gate, offs, out):
             elif item[0] == "bias":
                 nc.sync.dma_start(bias[:], b.rearrange("(h p) e -> p h e", p=P))
             elif item[0] == "gate":
-                nc.sync.dma_start(gate_all[:], gate.rearrange("(h p) j -> p h j", p=P))
+                q = item[1]
+                nc.sync.dma_start(gate_pair[q][:], gate.rearrange("(h p) j -> p h j", p=P)[:, :, q * 2 * C : (q + 1) * 2 * C])
             else:
                 e = item[1]
                 w_view = w[e].rearrange("(g p j) n -> p g j n", p=P, j=PACK)
-                if e < 2:
-                    for g in range(PASSES):
-                        half = held.tile(
-                            [P, PACK, N], F32, name="w_raw%d_%d" % (e, g), tag="w_raw%d_%d" % (e, g), align_bytes=64
-                        )
-                        nc.sync.dma_start(half[:], w_view[:, g])
-                        w_raw[e, g] = half[:]
-                else:
-                    whole = held.tile([P, PASSES, PACK, N], F32, name="w_raw%d" % e, tag="w_raw%d" % e, align_bytes=64)
-                    nc.sync.dma_start(whole[:], w_view)
-                    for g in range(PASSES):
-                        w_raw[e, g] = whole[:, g]
+                for g in range(PASSES):
+                    half = held.tile(
+                        [P, PACK, N], F32, name="w_raw%d_%d" % (e, g), tag="w_raw%d_%d" % (e, g), align_bytes=64
+                    )
+                    nc.sync.dma_start(half[:], w_view[:, g])
+                    w_raw[e, g] = half[:]
 
         window = {}
         for h in range(NB):
@@ -88,7 +83,7 @@ def tile_routed_moe_kernel(tc, xT, w, b, gate, offs, out):
         w_q = {}
         w_s = {}
         y = {}
-        y_tag = {(0, 0): "w_raw1_0", (0, 1): "w_raw1_1", (1, 0): "w_raw2", (1, 1): "w_raw3"}
+        y_tag = {(0, 0): "w_raw1_0", (0, 1): "w_raw1_1", (1, 0): "w_raw2_1", (1, 1): "w_raw3_1"}
         y_pair = [held.tile([P, 2 * C], F32, name="y_pair%d" % h) for h in range(NB)]
         for e in range(E):
             x_bf[e] = held.tile([P, PASSES, C, PACK], BF16, name="x_bf%d" % e, tag="x_bf%d" % e, align_bytes=64)
@@ -200,7 +195,7 @@ def tile_routed_moe_kernel(tc, xT, w, b, gate, offs, out):
             nc.vector.tensor_tensor(
                 window[h][:].indirect(offsets[:, e * (C // 16) : (e + 1) * (C // 16)]),
                 y[e, h],
-                gate_all[:, h, e * C : (e + 1) * C],
+                gate_pair[e // 2][:, h, (e % 2) * C : (e % 2 + 1) * C],
                 MULT,
             )
 
@@ -208,7 +203,7 @@ def tile_routed_moe_kernel(tc, xT, w, b, gate, offs, out):
             nc.vector.tensor_tensor(
                 window[h][:].indirect(offsets[:, 2 * (C // 16) : 4 * (C // 16)]),
                 y_pair[h][:],
-                gate_all[:, h, 2 * C : 4 * C],
+                gate_pair[1][:, h, :],
                 MULT,
             )
 
@@ -263,7 +258,8 @@ def tile_routed_moe_kernel(tc, xT, w, b, gate, offs, out):
         multiply(3, 0)
         multiply(3, 1)
         scatter(1, 1)
-        scatter_pair(0)
+        scatter(2, 0)
+        scatter(3, 0)
         store(0)
         scatter_pair(1)
         store(1)

from contextlib import ExitStack

import concourse.mybir as mybir

K, T, E, C, N = 1024, 2048, 4, 256, 256
SLOTS = E * C
FLOPS = 2 * K * N * SLOTS

F32 = mybir.dt.float32
BF16 = mybir.dt.bfloat16
U32 = mybir.dt.uint32
U16 = mybir.dt.uint16
U8 = mybir.dt.uint8
FP8X4 = mybir.dt.float8_e4m3fn_x4
MULT = mybir.AluOpType.mult
ADD = mybir.AluOpType.add
GELU = mybir.ActivationFunctionType.Gelu_apprx_tanh
COPY = mybir.ActivationFunctionType.Copy

P = 128
PACK = 4
K_PASS = P * PACK
PASSES = K // K_PASS
NB = N // P

LOAD_ORDER = (
    ("x", 0, 2), ("offs",), ("x", 0, 3), ("x", 1, 0), ("x", 0, 0), ("x", 0, 1), ("x", 1, 1), ("x", 1, 2), ("x", 1, 3),
    ("w", 0), ("bias",), ("gate", 0), ("w", 1), ("w", 2), ("w", 3), ("gate", 1),
)
S_PLANES = (0, 1)


def tile_routed_moe_kernel(tc, xT, w, b, gate, offs, out):
    nc = tc.nc
    with ExitStack() as ctx:
        lists = ctx.enter_context(tc.tile_pool(name="lists", bufs=1))
        held = ctx.enter_context(tc.tile_pool(name="held", bufs=1))
        psum = ctx.enter_context(tc.psum_pool(name="psum", bufs=1))

        offsets = lists.tile([P, SLOTS // 16], U16, name="offsets")
        bias = held.tile([P, NB, E], F32, name="bias")

        x_planes = xT.rearrange("(g p t) n -> g p t n", p=P, t=PACK)
        plane = {}
        w_raw = {}
        gate_pair = [held.tile([P, NB, 2 * C], F32, name="gate_pair%d" % q) for q in range(E // 2)]
        for item in LOAD_ORDER:
            if item[0] == "x":
                g, t = item[1], item[2]
                plane[g, t] = held.tile([P, T], F32, name="plane%d%d" % (g, t))
                nc.sync.dma_start(plane[g, t][:], x_planes[g, :, t, :])
            elif item[0] == "offs":
                nc.sync.dma_start(offsets[:], offs)
            elif item[0] == "bias":
                nc.sync.dma_start(bias[:], b.rearrange("(h p) e -> p h e", p=P))
            elif item[0] == "gate":
                q = item[1]
                nc.sync.dma_start(gate_pair[q][:], gate.rearrange("(h p) j -> p h j", p=P)[:, :, q * 2 * C : (q + 1) * 2 * C])
            else:
                e = item[1]
                w_view = w[e].rearrange("(g p j) n -> p g j n", p=P, j=PACK)
                for g in range(PASSES):
                    half = held.tile(
                        [P, PACK, N], F32, name="w_raw%d_%d" % (e, g), tag="w_raw%d_%d" % (e, g), align_bytes=64
                    )
                    nc.sync.dma_start(half[:], w_view[:, g])
                    w_raw[e, g] = half[:]

        window = {}
        for h in range(NB):
            window[h] = held.tile([P, T], F32, name="window%d" % h)
            nc.vector.memset(window[h][:], 0.0)
        warm = held.tile([P, 2], F32, name="warm")
        nc.gpsimd.memset(warm[:, 0:1], 0.0)
        nc.scalar.activation(out=warm[:, 1:2], in_=warm[:, 0:1], func=GELU)

        g4 = {}
        x_bf = {}
        x_q = {}
        x_s = {}
        w_bf = {}
        w_bf_whole = {}
        w_q = {}
        w_s = {}
        y = {}
        y_tag = {(0, 0): "w_raw1_0", (0, 1): "w_raw1_1", (1, 0): "w_raw2_1", (1, 1): "w_raw3_1"}
        y_pair = [held.tile([P, 2 * C], F32, name="y_pair%d" % h) for h in range(NB)]
        for e in range(E):
            x_bf[e] = held.tile([P, PASSES, C, PACK], BF16, name="x_bf%d" % e, tag="x_bf%d" % e, align_bytes=64)
        x_16 = held.tile([P, len(S_PLANES), T], BF16, name="x_16")
        g4[0, 1] = held.tile([P, 2, SLOTS], F32, name="g4_0_1")
        g4[1, 0] = held.tile([P, 2, SLOTS], F32, name="g4_1_0")
        g4[1, 1] = held.tile([P, 2, SLOTS], F32, name="g4_1_1", tag="late", align_bytes=64)

        def gather(g, t, e0, n_e):
            nc.vector.tensor_copy(
                g4[g, t // 2][:, t % 2, e0 * C : (e0 + n_e) * C],
                plane[g, t][:].indirect(offsets[:, e0 * (C // 16) : (e0 + n_e) * (C // 16)]),
            )

        def interleave(g, e, t0, n_t, engine="scalar"):
            picked = g4[g, t0 // 2][:, :, e * C : (e + 1) * C]
            if engine == "gpsimd":
                nc.gpsimd.tensor_scalar(
                    x_bf[e][:, g, :, t0 : t0 + n_t],
                    picked.rearrange("p t c -> p c t"),
                    1.0,
                    0.0,
                    MULT,
                    ADD,
                )
            else:
                nc.scalar.copy(
                    out=x_bf[e][:, g, :, t0 : t0 + n_t].rearrange("p (c i) t -> p c t i", i=4),
                    in_=picked.rearrange("p t (c i) -> p c t i", i=4),
                )

        def cast_plane(t):
            nc.gpsimd.tensor_scalar(x_16[:, t, :], plane[0, t][:], 1.0, 0.0, MULT, ADD)

        def gather_scalar(t, e):
            nc.scalar.activation(
                out=x_bf[e][:, 0, :, t],
                in_=x_16[:, t, :].indirect(offsets[:, e * (C // 16) : (e + 1) * (C // 16)]),
                func=COPY,
            )

        def quant_x(e):
            x_q[e] = held.tile([P, PASSES, C], U32, name="x_q%d" % e, align_bytes=64)
            x_s[e] = held.tile([P, PASSES, C], U8, name="x_s%d" % e, align_bytes=64)
            nc.vector.quantize_mx(
                out=x_q[e][:].rearrange("p g n -> p (g n)").bitcast(FP8X4),
                scales=x_s[e][:].rearrange("p g n -> p (g n)"),
                in_=x_bf[e][:].rearrange("p g n t -> p (g n t)"),
            )

        def alloc_w_bf(e, tags):
            if tags[0] == tags[1]:
                whole = held.tile([P, PASSES, N, PACK], BF16, name="w_bf%d" % e, tag=tags[0], align_bytes=64)
                w_bf[e] = [whole[:, g] for g in range(PASSES)]
                w_bf_whole[e] = whole
            else:
                halves = [
                    held.tile([P, N, PACK], BF16, name="w_bf%d_%d" % (e, g), tag=tags[g], align_bytes=64)
                    for g in range(PASSES)
                ]
                w_bf[e] = [half[:] for half in halves]

        def copy_w(e, g, engine):
            if engine == "scalar":
                nc.scalar.copy(
                    out=w_bf[e][g].rearrange("p (c i) j -> p c j i", i=4),
                    in_=w_raw[e, g].rearrange("p j (c i) -> p c j i", i=4),
                )
            else:
                nc.gpsimd.tensor_scalar(w_bf[e][g], w_raw[e, g].rearrange("p j n -> p n j"), 1.0, 0.0, MULT, ADD)

        def quant_w(e, tag):
            w_q[e] = held.tile([P, PASSES, N], U32, name="w_q%d" % e, tag=tag, align_bytes=64)
            w_s[e] = held.tile([P, PASSES, N], U8, name="w_s%d" % e, align_bytes=64)
            if e in w_bf_whole:
                nc.vector.quantize_mx(
                    out=w_q[e][:].rearrange("p g n -> p (g n)").bitcast(FP8X4),
                    scales=w_s[e][:].rearrange("p g n -> p (g n)"),
                    in_=w_bf_whole[e][:].rearrange("p g n j -> p (g n j)"),
                )
            else:
                for g in range(PASSES):
                    nc.vector.quantize_mx(
                        out=w_q[e][:, g, :].bitcast(FP8X4),
                        scales=w_s[e][:, g, :],
                        in_=w_bf[e][g].rearrange("p n j -> p (n j)"),
                    )

        def multiply(e, h):
            acc = psum.tile([P, C], F32, name="acc_%d_%d" % (e, h))
            for g in range(PASSES):
                nc.tensor.matmul_mx(
                    out=acc[:],
                    lhsT=w_q[e][:, g, h * P : (h + 1) * P].bitcast(FP8X4),
                    lhsT_scale=w_s[e][:, g, h * P : (h + 1) * P],
                    rhs=x_q[e][:, g, :].bitcast(FP8X4),
                    rhs_scale=x_s[e][:, g, :],
                    start=(g == 0),
                    stop=(g == PASSES - 1),
                )
            if e < 2:
                y_tile = held.tile([P, C], F32, name="y_%d_%d" % (e, h), tag=y_tag.get((e, h), "y_%d_%d" % (e, h)), align_bytes=64)
                y[e, h] = y_tile[:]
            else:
                y[e, h] = y_pair[h][:, (e - 2) * C : (e - 1) * C]
            nc.scalar.activation(out=y[e, h], in_=acc[:], func=GELU, bias=bias[:, h, e : e + 1])

        def scatter(e, h):
            nc.vector.tensor_tensor(
                window[h][:].indirect(offsets[:, e * (C // 16) : (e + 1) * (C // 16)]),
                y[e, h],
                gate_pair[e // 2][:, h, (e % 2) * C : (e % 2 + 1) * C],
                MULT,
            )

        def scatter_pair(h):
            nc.vector.tensor_tensor(
                window[h][:].indirect(offsets[:, 2 * (C // 16) : 4 * (C // 16)]),
                y_pair[h][:],
                gate_pair[1][:, h, :],
                MULT,
            )

        def store(h):
            nc.sync.dma_start(out[h * P : (h + 1) * P, :], window[h][:])

        for t in (2, 3):
            gather(0, t, 0, E)
        for e in range(E):
            interleave(0, e, 2, 2)
        gather(1, 0, 0, E)
        cast_plane(0)
        for e in range(E):
            gather_scalar(0, e)
        cast_plane(1)
        for e in range(E):
            gather_scalar(1, e)
        gather(1, 1, 0, E)
        for e in range(E):
            interleave(1, e, 0, 2, "gpsimd")
        gather(1, 2, 0, E)
        for e in range(E):
            gather(1, 3, e, 1)
            interleave(1, e, 2, 2)
        for e in range(E):
            quant_x(e)
        alloc_w_bf(0, ("w_bf0", "late"))
        copy_w(0, 0, "gpsimd")
        copy_w(0, 1, "scalar")
        quant_w(0, "w_q0")
        alloc_w_bf(1, ("x_bf0", "x_bf1"))
        copy_w(1, 0, "scalar")
        multiply(0, 0)
        copy_w(1, 1, "scalar")
        multiply(0, 1)
        scatter(0, 0)
        quant_w(1, "x_bf3")
        alloc_w_bf(2, ("w_bf0", "w_bf0"))
        copy_w(2, 0, "scalar")
        copy_w(2, 1, "scalar")
        multiply(1, 0)
        scatter(0, 1)
        quant_w(2, "w_q2")
        alloc_w_bf(3, ("w_bf1", "w_bf1"))
        copy_w(3, 0, "scalar")
        copy_w(3, 1, "scalar")
        multiply(1, 1)
        scatter(1, 0)
        quant_w(3, "x_bf2")
        multiply(2, 0)
        multiply(2, 1)
        multiply(3, 0)
        multiply(3, 1)
        scatter(1, 1)
        scatter(2, 0)
        scatter(3, 0)
        store(0)
        scatter_pair(1)
        store(1)
